import numpy as np
import ml_dtypes


def mxq(x, axis, fmt="e4m3"):
    dtype, down = {"e4m3": (ml_dtypes.float8_e4m3fn, 7), "e5m2": (ml_dtypes.float8_e5m2, 14)}[fmt]
    v = np.moveaxis(np.asarray(x, np.float32).astype(ml_dtypes.bfloat16).astype(np.float64), axis, -1)
    blocks = v.reshape(v.shape[:-1] + (-1, 32))
    amax = np.abs(blocks).max(-1, keepdims=True)
    byte = np.maximum(np.where(amax > 0, np.frexp(amax)[1] - 1 + 127, 0) - down, 1)
    scale = np.exp2(byte - 127.0)
    codes = (blocks / scale).astype(np.float32).astype(dtype).astype(np.float64)
    return np.moveaxis((codes * scale).reshape(v.shape), -1, axis)


WIDE = False


def mx_kscale(k):
    if not WIDE:
        return np.ones(k)
    levels = np.array([10, -10, 5, -5, 0])
    if k % 512:
        return np.exp2(np.random.permutation(np.resize(levels, k // 32))).repeat(32)
    a = np.empty((k // 512, 16))
    for p in range(k // 512):
        a[p, :8] = np.random.permutation(np.resize(levels, 8))
        for g in range(8):
            far = levels[np.abs(levels - a[p, g]) >= 10]
            a[p, g + 8] = far[np.random.randint(len(far))]
    return np.exp2(a.ravel()).repeat(32)


BF16 = ml_dtypes.bfloat16


def bf(x):
    return np.asarray(x, np.float32).astype(BF16)


def f64(x):
    return np.asarray(x).astype(np.float64)


E2M1 = np.array([0.0, 0.5, 1.0, 1.5, 2.0, 3.0, 4.0, 6.0, -0.0, -0.5, -1.0, -1.5, -2.0, -3.0, -4.0, -6.0])


def pack_weight(w, fmt):
    k, n = w.shape
    w = f64(bf(w)).reshape(k // 32, 32, n)
    amax = np.abs(w).max(1)
    if fmt == "e4m3":
        byte = np.frexp(amax)[1] - 1 + 127 - 7
    else:
        mant, ex = np.frexp(amax / 6.0)
        byte = np.where(mant > 0.5, ex, ex - 1) + 127
    byte = np.clip(np.where(amax > 0, byte, 1), 1, 254)
    scaled = (w * np.exp2(127.0 - byte)[:, None, :]).reshape(k, n).astype(np.float32)
    by_word = np.ascontiguousarray(scaled.reshape(k // 512, 128, 4, n).transpose(0, 1, 3, 2))
    if fmt == "e4m3":
        words = by_word.astype(ml_dtypes.float8_e4m3fn).view(np.uint8)
    else:
        c = by_word.astype(ml_dtypes.float4_e2m1fn).view(np.uint8) & 0xF
        words = c[..., 0::2] | (c[..., 1::2] << 4)
    return np.ascontiguousarray(words), np.ascontiguousarray(byte.astype(np.uint8).reshape(k // 512, 16, n))


def unpack_weight(words, scales, fmt):
    g, p, n, _ = words.shape
    if fmt == "e4m3":
        vals = np.ascontiguousarray(words).view(ml_dtypes.float8_e4m3fn).astype(np.float64)
    else:
        nib = np.empty((g, p, n, 4), np.uint8)
        nib[..., 0::2] = words & 0xF
        nib[..., 1::2] = words >> 4
        vals = E2M1[nib]
    vals = vals * np.repeat(np.exp2(scales.astype(np.float64) - 127.0), 8, axis=1)[..., None]
    return vals.transpose(0, 1, 3, 2).reshape(g * 512, n)
def pack4(w):
    words, scales = pack_weight(w, "e2m1")
    return words.reshape(words.shape[0], 128, -1), scales


def unpack4(words, scales):
    return unpack_weight(words.reshape(words.shape[0], 128, -1, 2), scales, "e2m1")


def planes(Y):
    n, m = Y.shape
    b = f64(bf(Y)).reshape(n // 32, 32, m)
    amax = np.abs(b).max(1)
    byte = np.clip(np.where(amax > 0, np.frexp(amax)[1] - 1 + 127 - 7, 1), 1, 254)
    codes = (b * np.exp2(127.0 - byte)[:, None, :]).reshape(n, m).astype(np.float32).astype(ml_dtypes.float8_e4m3fn).view(np.uint8)
    words = codes.reshape(n // 512, 128, 4, m).transpose(0, 1, 3, 2)
    return np.ascontiguousarray(words), np.ascontiguousarray(byte.astype(np.uint8).reshape(n // 512, 16, m))


N, D, F = 1024, 1024, 1024


def sigmoid(a):
    return 1.0 / (1.0 + np.exp(-a))


def silu(a):
    return a * sigmoid(a)


def silu_grad(a):
    s = sigmoid(a)
    return s * (1.0 + a * (1.0 - s))


def setup_inputs():
    s = mx_kscale(D)
    uc, ur = mx_kscale(N), mx_kscale(N)
    hc = bf(np.random.standard_normal((N, D)) * s[None, :] * uc[:, None])
    hr = bf(np.random.standard_normal((N, D)) * s[None, :] * ur[:, None])
    w1_words, w1_scales = pack4(np.random.standard_normal((D, F)) / np.sqrt(D) / s[:, None])
    return {
        "hc": hc,
        "hr": hr,
        "w1_words": w1_words,
        "w1_scales": w1_scales,
        "v": bf(np.random.standard_normal(F)),
        "sc": bf((1.0 + 0.1 * np.random.standard_normal(N)) / uc),
        "sr": bf((1.0 + 0.1 * np.random.standard_normal(N)) / ur),
        "m": bf(np.random.uniform(0.0, 1.0, N)),
    }


def core(hc, hr, w1_words, w1_scales, v, sc, sr, m):
    hc, hr, v, sc, sr, m = f64(hc), f64(hr), f64(v), f64(sc), f64(sr), f64(m)
    inv_sqrt_f = 1.0 / np.sqrt(F)

    w1q = unpack4(w1_words, w1_scales)
    ac = sc[:, None] * (mxq(hc, 1, "e4m3") @ w1q)
    ar = sr[:, None] * (mxq(hr, 1, "e4m3") @ w1q)

    rc = inv_sqrt_f * np.sum(silu(ac) * v[None, :], axis=-1)
    rr = inv_sqrt_f * np.sum(silu(ar) * v[None, :], axis=-1)

    k = -sigmoid(m + rr - rc)

    gc = k[:, None] * v[None, :] * silu_grad(ac) * sc[:, None]
    gr = -k[:, None] * v[None, :] * silu_grad(ar) * sr[:, None]

    pc = mxq(hc, 0, "e4m3").T @ mxq(gc, 0, "e4m3")
    pr = mxq(hr, 0, "e4m3").T @ mxq(gr, 0, "e4m3")
    return inv_sqrt_f * (pc + pr)


def reference(hc, hr, w1_words, w1_scales, v, sc, sr, m):
    R_out = core(hc, hr, w1_words, w1_scales, v, sc, sr, m)
    words, scales = planes(R_out)
    return R_out, words, scales

@@ -1,0 +1,354 @@
+from contextlib import ExitStack
+
+import concourse.mybir as mybir
+from concourse.masks import make_identity
+
+N, D, F = 1024, 1024, 1024
+FLOPS = 4 * 2 * N * D * F
+
+F32 = mybir.dt.float32
+BF16 = mybir.dt.bfloat16
+I32 = mybir.dt.int32
+U32 = mybir.dt.uint32
+U8 = mybir.dt.uint8
+FP8X4 = mybir.dt.float8_e4m3fn_x4
+FP4X4 = mybir.dt.float4_e2m1fn_x4
+ALU = mybir.AluOpType
+ACT = mybir.ActivationFunctionType
+
+P = 128
+PACK = 4
+GROUPS = 2
+BLOCKS = 4
+TILES = BLOCKS * PACK
+BANK = 512
+INV_SQRT_F = 1.0 / 32.0
+CHUNK = 256
+CHUNKS = F // CHUNK
+PIECES = 4
+RUN = 4
+
+
+def tile_marginbradleyterryrewardmlpweightgradien_x2_kernel(
+    tc, hc, hr, w1_words, w1_scales, v, sc, sr, m, out_0, out_1, out_2
+):
+    nc = tc.nc
+    h_dram = (hc, hr)
+    s_dram = (sc, sr)
+
+    with ExitStack() as ctx:
+        sb = ctx.enter_context(tc.tile_pool(name="sb", bufs=1))
+        ps = ctx.enter_context(tc.psum_pool(name="ps", bufs=1))
+        ctx.enter_context(tc.manual_schedule())
+
+        def ring(name, count, shape, dtype):
+            return [sb.tile(shape, dtype, name="%s%d" % (name, i), align_bytes=64) for i in range(count)]
+
+        banks = [ps.tile([P, BANK], F32, name="bank%d" % i) for i in range(8)]
+        raw = ring("raw", BLOCKS, [P, PACK, D], BF16)
+        w_words = sb.tile([P, GROUPS, 2 * F], U8, align_bytes=64)
+        w_scales = sb.tile([P, GROUPS, F], U8, align_bytes=64)
+        ident = sb.tile([P, P], F32, align_bytes=64)
+        ones = sb.tile([P, P], BF16, align_bytes=64)
+        v_row = sb.tile([P, F], BF16, align_bytes=64)
+        s_bf = ring("s_bf", 2, [P, GROUPS, PACK], BF16)
+        m_bf = sb.tile([P, GROUPS, PACK], BF16, align_bytes=64)
+        s_full = ring("s_full", 2, [P, GROUPS * PACK], F32)
+        s_half = ring("s_half", 2, [P, GROUPS * PACK], F32)
+        s_signed = sb.tile([P, 2, GROUPS * PACK], F32, align_bytes=64)
+        sums = sb.tile([P, 2, GROUPS * PACK], F32, align_bytes=64)
+        part = sb.tile([P, GROUPS * PACK], F32, align_bytes=64)
+        logit = sb.tile([P, GROUPS * PACK], F32, align_bytes=64)
+        sig = sb.tile([P, GROUPS * PACK], F32, align_bytes=64)
+        row_factor = sb.tile([P, 2, GROUPS * PACK], F32, align_bytes=64)
+        ht = ring("ht", 2, [P, GROUPS * P * PACK], BF16)
+        ht_codes = ring("ht_codes", 4, [P, GROUPS * P], U32)
+        ht_scales = ring("ht_scales", 4, [P, GROUPS * P], U8)
+        hn = ring("hn", 2, [P, D * PACK], BF16)
+        hn_codes = ring("hn_codes", BLOCKS, [P, D], U32)
+        hn_scales = ring("hn_scales", BLOCKS, [P, D], U8)
+        u_t = ring("u_t", 3, [P, F], F32)
+        t_t = ring("t_t", 3, [P, F], F32)
+        y_t = ring("y_t", BLOCKS, [P, PACK, F], F32)
+        g_bf = ring("g_bf", 3, [P, CHUNK * PACK], BF16)
+        g_codes = ring("g_codes", 3, [P, CHUNK], U32)
+        g_scales = ring("g_scales", 3, [P, CHUNK], U8)
+        o_f32 = ring("o_f32", 4, [P, PACK, CHUNK], F32)
+        o_bf = ring("o_bf", 3, [P, CHUNK * PACK], BF16)
+        o_codes = sb.tile([P, GROUPS, F], U32, align_bytes=64)
+        o_scales = sb.tile([P, GROUPS, F], U8, align_bytes=64)
+
+        v_all = banks[7][:].bitcast(BF16)
+
+        def t_bank(t):
+            return banks[2 * t] if t in (1, 2) else banks[6]
+
+        def side_of(b):
+            return b % 2
+
+        def col_of(t):
+            return (t // PACK // 2) * PACK + t % PACK
+
+        def load_rows(b, j0, j1):
+            rows = h_dram[side_of(b)][(b // 2) * 512 : (b // 2 + 1) * 512, :].rearrange("(p j) d -> p j d", j=PACK)
+            nc.sync.dma_start(out=raw[b][:, j0:j1, :], in_=rows[:, j0:j1, :])
+
+        def transposes(t):
+            words = raw[t // PACK][:, t % PACK, :].bitcast(F32)
+            bank = t_bank(t)
+            for g in range(GROUPS):
+                for u in range(2):
+                    q = 2 * g + u
+                    nc.tensor.transpose(
+                        bank[:, q * P : (q + 1) * P], words[:, 256 * g + u : 256 * (g + 1) : 2], ident[:]
+                    )
+
+        def unload_t(t, on_vector):
+            src = t_bank(t)[:].rearrange("p (g u n) -> p g n u", g=GROUPS, u=2)
+            dst = ht[t % 2][:].bitcast(F32).rearrange("p (g n u) -> p g n u", g=GROUPS, u=2)
+            if on_vector:
+                nc.vector.tensor_copy(out=dst, in_=src)
+            else:
+                nc.scalar.copy(out=dst, in_=src)
+
+        def quant_t(t):
+            nc.vector.quantize_mx(out=ht_codes[t % 4][:].bitcast(FP8X4), scales=ht_scales[t % 4][:], in_=ht[t % 2][:])
+
+        def forward(t):
+            for half in range(2):
+                for g in range(GROUPS):
+                    nc.tensor.matmul_mx(
+                        out=banks[2 * (t % 3) + half][:],
+                        lhsT=ht_codes[t % 4][:, g * P : (g + 1) * P].bitcast(FP8X4),
+                        lhsT_scale=ht_scales[t % 4][:, g * P : (g + 1) * P],
+                        rhs=w_words[:, g, 2 * BANK * half : 2 * BANK * (half + 1)].bitcast(FP4X4),
+                        rhs_scale=w_scales[:, g, BANK * half : BANK * (half + 1)],
+                        start=(g == 0),
+                        stop=(g == GROUPS - 1),
+                    )
+
+        def activate(t, func, dst, scales):
+            c = col_of(t)
+            for half in range(2):
+                nc.scalar.activation(
+                    out=dst[t % 3][:, BANK * half : BANK * (half + 1)],
+                    in_=banks[2 * (t % 3) + half][:],
+                    func=func,
+                    scale=scales[side_of(t // PACK)][:, c : c + 1],
+                )
+
+        def op_w(t):
+            c = col_of(t)
+            nc.vector.scalar_tensor_tensor(
+                out=u_t[t % 3][:], in0=u_t[t % 3][:], scalar=1.0, in1=v_all, op0=ALU.subtract, op1=ALU.mult,
+                accum_out=sums[:, side_of(t // PACK), c : c + 1],
+            )
+
+        def op_x(t):
+            nc.vector.scalar_tensor_tensor(
+                out=t_t[t % 3][:], in0=t_t[t % 3][:], scalar=1.0, in1=u_t[t % 3][:], op0=ALU.subtract, op1=ALU.mult
+            )
+
+        def op_y(t):
+            nc.vector.scalar_tensor_tensor(
+                out=y_t[t // PACK][:, t % PACK, :], in0=t_t[t % 3][:], scalar=-0.5, in1=v_all,
+                op0=ALU.mult, op1=ALU.add,
+            )
+
+        def weave_h(piece):
+            b, q = divmod(piece, PIECES)
+            g, half = divmod(q, 2)
+            ms = slice(64 * half, 64 * (half + 1))
+            src = raw[b][:, :, 512 * g : 512 * (g + 1)].rearrange("p j (m t) -> p m t j", t=PACK)
+            dst = hn[b % 2][:, 2048 * g : 2048 * (g + 1)].rearrange("p (t m j) -> p m t j", t=PACK, j=PACK)
+            nc.scalar.copy(out=dst[:, ms, :, :], in_=src[:, ms, :, :])
+
+        def quant_h(b):
+            nc.vector.quantize_mx(out=hn_codes[b][:].bitcast(FP8X4), scales=hn_scales[b][:], in_=hn[b % 2][:])
+
+        def make_g(q):
+            c, b = divmod(q, BLOCKS)
+            cols = slice(CHUNK * c, CHUNK * (c + 1))
+            k4 = row_factor[:, side_of(b), PACK * (b // 2) : PACK * (b // 2 + 1)]
+            nc.vector.tensor_tensor(
+                out=g_bf[q % 3][:].rearrange("p (c i j) -> p c j i", i=RUN, j=PACK),
+                in0=y_t[b][:, :, cols].rearrange("p j (c i) -> p c j i", i=RUN),
+                in1=k4.rearrange("p (a j e) -> p a j e", a=1, e=1).to_broadcast([P, CHUNK // RUN, PACK, RUN]),
+                op=ALU.mult,
+            )
+
+        def quant_g(q):
+            nc.vector.quantize_mx(out=g_codes[q % 3][:].bitcast(FP8X4), scales=g_scales[q % 3][:], in_=g_bf[q % 3][:])
+
+        def backward(q):
+            b = q % BLOCKS
+            for i in range(8):
+                nc.tensor.matmul_mx(
+                    out=banks[i][:, 0:CHUNK],
+                    lhsT=hn_codes[b][:, i * P : (i + 1) * P].bitcast(FP8X4),
+                    lhsT_scale=hn_scales[b][:, i * P : (i + 1) * P],
+                    rhs=g_codes[q % 3][:].bitcast(FP8X4),
+                    rhs_scale=g_scales[q % 3][:],
+                    start=(b == 0),
+                    stop=(b == BLOCKS - 1),
+                )
+
+        def unload_out(r, on_vector):
+            c, g = divmod(r, GROUPS)
+            for t in range(PACK):
+                if on_vector:
+                    nc.vector.tensor_scalar(
+                        out=o_f32[r % 4][:, t, :], in0=banks[PACK * g + t][:, 0:CHUNK],
+                        scalar1=INV_SQRT_F, scalar2=None, op0=ALU.mult,
+                    )
+                else:
+                    nc.scalar.activation(
+                        out=o_f32[r % 4][:, t, :], in_=banks[PACK * g + t][:, 0:CHUNK], func=ACT.Copy, scale=INV_SQRT_F
+                    )
+            rows = out_0[512 * g : 512 * (g + 1), CHUNK * c : CHUNK * (c + 1)].rearrange("(p t) f -> p t f", t=PACK)
+            nc.sync.dma_start(out=rows, in_=o_f32[r % 4][:])
+
+        def weave_out(r, on_vector):
+            src = o_f32[r % 4][:].rearrange("p t (c i) -> p c t i", i=RUN)
+            dst = o_bf[r % 3][:].rearrange("p (c i t) -> p c t i", i=RUN, t=PACK)
+            if on_vector:
+                nc.vector.tensor_copy(out=dst, in_=src)
+            else:
+                nc.scalar.copy(out=dst, in_=src)
+
+        def quant_out(r):
+            c, g = divmod(r, GROUPS)
+            cols = slice(CHUNK * c, CHUNK * (c + 1))
+            nc.vector.quantize_mx(
+                out=o_codes[:, g, cols].bitcast(FP8X4), scales=o_scales[:, g, cols], in_=o_bf[r % 3][:]
+            )
+            words = out_1[g].rearrange("p f t -> p (f t)")[:, PACK * CHUNK * c : PACK * CHUNK * (c + 1)]
+            nc.sync.dma_start(out=words.bitcast(I32), in_=o_codes[:, g, cols].bitcast(I32))
+
+        def load_vector(queue, dst, vec):
+            queue.dma_start(out=dst[:], in_=vec.rearrange("(g p j) -> p g j", g=GROUPS, j=PACK))
+
+        def row_scales(side):
+            flat = s_bf[side][:].rearrange("p g j -> p (g j)")
+            for dst, factor in (
+                (s_full[side][:], 1.0),
+                (s_half[side][:], 0.5),
+                (s_signed[:, side, :], 2.0 * side - 1.0),
+            ):
+                nc.vector.tensor_scalar(out=dst, in0=flat, scalar1=factor, scalar2=None, op0=ALU.mult)
+
+        nc.vector.memset(w_scales[:].rearrange("p g n -> p (g n)").bitcast(I32), 0)
+        nc.vector.memset(v_row[:], 0.0)
+        nc.vector.memset(ones[:], 1.0)
+        make_identity(nc, ident[:])
+        load_rows(0, 0, 1)
+        load_vector(nc.scalar, s_bf[0], sc)
+        nc.sync.dma_start(
+            out=w_words[:].bitcast(I32), in_=w1_words.rearrange("g p n -> p g n").bitcast(I32)
+        )
+        for q in range(4):
+            nc.scalar.dma_start(
+                out=w_scales[32 * q : 32 * q + 4, :, :].bitcast(I32),
+                in_=w1_scales[:, 4 * q : 4 * q + 4, :].rearrange("g r n -> r g n").bitcast(I32),
+            )
+        for j in range(1, PACK):
+            load_rows(0, j, j + 1)
+        for b in range(1, BLOCKS):
+            load_rows(b, 0, 2)
+            load_rows(b, 2, 4)
+        nc.gpsimd.dma_start(out=v_row[0:1, :], in_=v.rearrange("(o f) -> o f", o=1))
+        load_vector(nc.gpsimd, s_bf[1], sr)
+        load_vector(nc.gpsimd, m_bf, m)
+
+        transposes(0)
+        transposes(1)
+        unload_t(0, True)
+        row_scales(0)
+        quant_t(0)
+        forward(0)
+        transposes(2)
+        for half in range(2):
+            cols = slice(BANK * half, BANK * (half + 1))
+            nc.tensor.matmul(v_all[:, cols], lhsT=ones[:], rhs=v_row[:, cols], start=True, stop=True)
+        transposes(3)
+        unload_t(1, True)
+        unload_t(2, True)
+        quant_t(1)
+        forward(1)
+        quant_t(2)
+        forward(2)
+        unload_t(3, True)
+        row_scales(1)
+
+        for s in range(TILES):
+            activate(s, ACT.Silu, u_t, s_full)
+            op_w(s)
+            if s >= 1:
+                op_y(s - 1)
+                if s + 3 < TILES:
+                    unload_t(s + 3, False)
+            if s + 4 < TILES:
+                transposes(s + 4)
+            if s + 3 < TILES:
+                quant_t(s + 3)
+            activate(s, ACT.Tanh, t_t, s_half)
+            if s + 3 < TILES:
+                forward(s + 3)
+            if s == TILES - 2:
+                nc.vector.scalar_tensor_tensor(
+                    out=part[:], in0=sums[:, 0, :], scalar=-INV_SQRT_F, in1=m_bf[:].rearrange("p g j -> p (g j)"),
+                    op0=ALU.mult, op1=ALU.add,
+                )
+            if s == TILES - 1:
+                nc.vector.scalar_tensor_tensor(
+                    out=logit[:], in0=sums[:, 1, :], scalar=INV_SQRT_F, in1=part[:], op0=ALU.mult, op1=ALU.add
+                )
+                nc.scalar.activation(out=sig[:], in_=logit[:], func=ACT.Sigmoid)
+            op_x(s)
+            if 2 <= s < 2 + 3 * PIECES:
+                weave_h(s - 2)
+            if s in (6, 10):
+                quant_h((s - 6) // PIECES)
+        quant_h(2)
+        op_y(TILES - 1)
+        nc.vector.tensor_tensor(
+            out=row_factor[:],
+            in0=s_signed[:],
+            in1=sig[:].rearrange("p (a c) -> p a c", a=1).to_broadcast([P, 2, GROUPS * PACK]),
+            op=ALU.mult,
+        )
+        for piece in range(3 * PIECES, 4 * PIECES):
+            weave_h(piece)
+
+        steps = CHUNKS * BLOCKS
+        for q in range(steps + 1):
+            c, b = divmod(q, BLOCKS)
+            if q < steps:
+                make_g(q)
+            if q == BLOCKS:
+                quant_h(BLOCKS - 1)
+            if q >= 1:
+                quant_g(q - 1)
+                backward(q - 1)
+            if b == 0 and 1 <= c < CHUNKS:
+                unload_out(2 * (c - 1), False)
+                unload_out(2 * (c - 1) + 1, False)
+                weave_out(2 * (c - 1), False)
+                weave_out(2 * (c - 1) + 1, False)
+            if b == 3 and c >= 1:
+                quant_out(2 * (c - 1))
+            if b == 0 and c >= 2:
+                quant_out(2 * (c - 2) + 1)
+        last = 2 * (CHUNKS - 1)
+        unload_out(last, False)
+        weave_out(last, False)
+        unload_out(last + 1, True)
+        weave_out(last + 1, True)
+        quant_out(last)
+        quant_out(last + 1)
+        for q in range(4):
+            queue = nc.scalar if q % 2 == 0 else nc.sync
+            queue.dma_start(
+                out=out_2[:, 4 * q : 4 * q + 4, :].rearrange("g r n -> r g n").bitcast(I32),
+                in_=o_scales[32 * q : 32 * q + 4, :, :].bitcast(I32),
+            )

@@ -24,9 +24,14 @@ TILES = BLOCKS * PACK
 BANK = 512
 INV_SQRT_F = 1.0 / 32.0
 CHUNK = 256
-CHUNKS = F // CHUNK
+WIDTHS = (256, 256, 256, 128, 128)
+G_RING = 8
+PLAN = "V-S-S-S-S-S-S-SS"
+LATE_QUANT = {2: 1, 3: 4}
+OUT_QUANT = {0: 8, 1: 9, 2: 12, 3: 13, 4: 18, 5: 19, 6: 20, 7: 20}
 PIECES = 4
 RUN = 4
+POOL_COLS = 640
 
 
 def tile_marginbradleyterryrewardmlpweightgradien_x2_kernel(
@@ -49,6 +54,8 @@ def tile_marginbradleyterryrewardmlpweightgradien_x2_kernel(
         w_words = sb.tile([P, GROUPS, 2 * F], U8, align_bytes=64)
         w_scales = sb.tile([P, GROUPS, F], U8, align_bytes=64)
         ident = sb.tile([P, P], F32, align_bytes=64)
+        v_pool = sb.tile([P, POOL_COLS], F32, align_bytes=64)
+        warm = sb.tile([P, 1], F32, align_bytes=64)
         ones = sb.tile([P, P], BF16, align_bytes=64)
         v_row = sb.tile([P, F], BF16, align_bytes=64)
         s_bf = ring("s_bf", 2, [P, GROUPS, PACK], BF16)
@@ -71,17 +78,17 @@ def tile_marginbradleyterryrewardmlpweightgradien_x2_kernel(
         t_t = ring("t_t", 3, [P, F], F32)
         y_t = ring("y_t", BLOCKS, [P, PACK, F], F32)
         g_bf = ring("g_bf", 3, [P, CHUNK * PACK], BF16)
-        g_codes = ring("g_codes", 3, [P, CHUNK], U32)
-        g_scales = ring("g_scales", 3, [P, CHUNK], U8)
+        g_codes = ring("g_codes", G_RING, [P, CHUNK], U32)
+        g_scales = ring("g_scales", G_RING, [P, CHUNK], U8)
         o_f32 = ring("o_f32", 4, [P, PACK, CHUNK], F32)
-        o_bf = ring("o_bf", 3, [P, CHUNK * PACK], BF16)
+        o_bf = ring("o_bf", 4, [P, CHUNK * PACK], BF16)
         o_codes = sb.tile([P, GROUPS, F], U32, align_bytes=64)
         o_scales = sb.tile([P, GROUPS, F], U8, align_bytes=64)
 
         v_all = banks[7][:].bitcast(BF16)
 
         def t_bank(t):
-            return banks[2 * t] if t in (1, 2) else banks[6]
+            return banks[2] if t == 1 else banks[6]
 
         def side_of(b):
             return b % 2
@@ -149,68 +156,85 @@ def tile_marginbradleyterryrewardmlpweightgradien_x2_kernel(
                 out=t_t[t % 3][:], in0=t_t[t % 3][:], scalar=1.0, in1=u_t[t % 3][:], op0=ALU.subtract, op1=ALU.mult
             )
 
-        def op_y(t):
+        def op_y(t, first):
             nc.vector.scalar_tensor_tensor(
-                out=y_t[t // PACK][:, t % PACK, :], in0=t_t[t % 3][:], scalar=-0.5, in1=v_all,
-                op0=ALU.mult, op1=ALU.add,
+                out=y_t[t // PACK][:, t % PACK, first:F], in0=v_all[:, first:F], scalar=2.0,
+                in1=t_t[t % 3][:, first:F], op0=ALU.mult, op1=ALU.subtract,
             )
 
-        def weave_h(piece):
+        def op_y_pool(t):
+            nc.gpsimd.tensor_tensor(
+                out=y_t[t // PACK][:, t % PACK, 0:POOL_COLS], in0=v_pool[:], in1=t_t[t % 3][:, 0:POOL_COLS],
+                op=ALU.subtract,
+            )
+
+        def weave_h(piece, on_vector):
             b, q = divmod(piece, PIECES)
             g, half = divmod(q, 2)
             ms = slice(64 * half, 64 * (half + 1))
             src = raw[b][:, :, 512 * g : 512 * (g + 1)].rearrange("p j (m t) -> p m t j", t=PACK)
             dst = hn[b % 2][:, 2048 * g : 2048 * (g + 1)].rearrange("p (t m j) -> p m t j", t=PACK, j=PACK)
-            nc.scalar.copy(out=dst[:, ms, :, :], in_=src[:, ms, :, :])
+            if on_vector:
+                nc.vector.tensor_copy(out=dst[:, ms, :, :], in_=src[:, ms, :, :])
+            else:
+                nc.scalar.copy(out=dst[:, ms, :, :], in_=src[:, ms, :, :])
 
         def quant_h(b):
             nc.vector.quantize_mx(out=hn_codes[b][:].bitcast(FP8X4), scales=hn_scales[b][:], in_=hn[b % 2][:])
 
+        def chunk_cols(c):
+            return slice(sum(WIDTHS[:c]), sum(WIDTHS[: c + 1]))
+
         def make_g(q):
             c, b = divmod(q, BLOCKS)
-            cols = slice(CHUNK * c, CHUNK * (c + 1))
+            width = WIDTHS[c]
             k4 = row_factor[:, side_of(b), PACK * (b // 2) : PACK * (b // 2 + 1)]
             nc.vector.tensor_tensor(
-                out=g_bf[q % 3][:].rearrange("p (c i j) -> p c j i", i=RUN, j=PACK),
-                in0=y_t[b][:, :, cols].rearrange("p j (c i) -> p c j i", i=RUN),
-                in1=k4.rearrange("p (a j e) -> p a j e", a=1, e=1).to_broadcast([P, CHUNK // RUN, PACK, RUN]),
+                out=g_bf[q % 3][:, 0 : PACK * width].rearrange("p (c i j) -> p c j i", i=RUN, j=PACK),
+                in0=y_t[b][:, :, chunk_cols(c)].rearrange("p j (c i) -> p c j i", i=RUN),
+                in1=k4.rearrange("p (a j e) -> p a j e", a=1, e=1).to_broadcast([P, width // RUN, PACK, RUN]),
                 op=ALU.mult,
             )
 
         def quant_g(q):
-            nc.vector.quantize_mx(out=g_codes[q % 3][:].bitcast(FP8X4), scales=g_scales[q % 3][:], in_=g_bf[q % 3][:])
+            width = WIDTHS[q // BLOCKS]
+            nc.vector.quantize_mx(
+                out=g_codes[q % G_RING][:, 0:width].bitcast(FP8X4),
+                scales=g_scales[q % G_RING][:, 0:width],
+                in_=g_bf[q % 3][:, 0 : PACK * width],
+            )
 
         def backward(q):
-            b = q % BLOCKS
+            c, b = divmod(q, BLOCKS)
+            width = WIDTHS[c]
             for i in range(8):
                 nc.tensor.matmul_mx(
-                    out=banks[i][:, 0:CHUNK],
+                    out=banks[i][:, 0:width],
                     lhsT=hn_codes[b][:, i * P : (i + 1) * P].bitcast(FP8X4),
                     lhsT_scale=hn_scales[b][:, i * P : (i + 1) * P],
-                    rhs=g_codes[q % 3][:].bitcast(FP8X4),
-                    rhs_scale=g_scales[q % 3][:],
+                    rhs=g_codes[q % G_RING][:, 0:width].bitcast(FP8X4),
+                    rhs_scale=g_scales[q % G_RING][:, 0:width],
                     start=(b == 0),
                     stop=(b == BLOCKS - 1),
                 )
 
         def unload_out(r, on_vector):
             c, g = divmod(r, GROUPS)
+            width = WIDTHS[c]
             for t in range(PACK):
+                dst = o_f32[r % 4][:, t, 0:width]
+                src = banks[PACK * g + t][:, 0:width]
                 if on_vector:
-                    nc.vector.tensor_scalar(
-                        out=o_f32[r % 4][:, t, :], in0=banks[PACK * g + t][:, 0:CHUNK],
-                        scalar1=INV_SQRT_F, scalar2=None, op0=ALU.mult,
-                    )
+                    nc.vector.tensor_scalar(out=dst, in0=src, scalar1=INV_SQRT_F, scalar2=None, op0=ALU.mult)
                 else:
-                    nc.scalar.activation(
-                        out=o_f32[r % 4][:, t, :], in_=banks[PACK * g + t][:, 0:CHUNK], func=ACT.Copy, scale=INV_SQRT_F
-                    )
-            rows = out_0[512 * g : 512 * (g + 1), CHUNK * c : CHUNK * (c + 1)].rearrange("(p t) f -> p t f", t=PACK)
-            nc.sync.dma_start(out=rows, in_=o_f32[r % 4][:])
+                    nc.scalar.activation(out=dst, in_=src, func=ACT.Copy, scale=INV_SQRT_F)
+            rows = out_0[512 * g : 512 * (g + 1), chunk_cols(c)].rearrange("(p t) f -> p t f", t=PACK)
+            nc.sync.dma_start(out=rows, in_=o_f32[r % 4][:, :, 0:width])
 
         def weave_out(r, on_vector):
-            src = o_f32[r % 4][:].rearrange("p t (c i) -> p c t i", i=RUN)
-            dst = o_bf[r % 3][:].rearrange("p (c i t) -> p c t i", i=RUN, t=PACK)
+            width = WIDTHS[r // GROUPS]
+            src = o_f32[r % 4][:, :, 0:width].rearrange("p t (c i) -> p c t i", i=RUN)
+            dst = o_bf[r % 4][:, 0 : PACK * width].rearrange("p (c i t) -> p c t i", i=RUN, t=PACK)
             if on_vector:
                 nc.vector.tensor_copy(out=dst, in_=src)
             else:
@@ -218,12 +242,16 @@ def tile_marginbradleyterryrewardmlpweightgradien_x2_kernel(
 
         def quant_out(r):
             c, g = divmod(r, GROUPS)
-            cols = slice(CHUNK * c, CHUNK * (c + 1))
+            cols = chunk_cols(c)
             nc.vector.quantize_mx(
-                out=o_codes[:, g, cols].bitcast(FP8X4), scales=o_scales[:, g, cols], in_=o_bf[r % 3][:]
+                out=o_codes[:, g, cols].bitcast(FP8X4),
+                scales=o_scales[:, g, cols],
+                in_=o_bf[r % 4][:, 0 : PACK * WIDTHS[c]],
             )
-            words = out_1[g].rearrange("p f t -> p (f t)")[:, PACK * CHUNK * c : PACK * CHUNK * (c + 1)]
-            nc.sync.dma_start(out=words.bitcast(I32), in_=o_codes[:, g, cols].bitcast(I32))
+            if g == GROUPS - 1 and cols.stop % CHUNK == 0:
+                done = slice(cols.stop - CHUNK, cols.stop)
+                words = out_1.rearrange("g p f t -> p g (f t)")[:, :, PACK * done.start : PACK * done.stop]
+                nc.sync.dma_start(out=words.bitcast(I32), in_=o_codes[:, :, done].bitcast(I32))
 
         def load_vector(queue, dst, vec):
             queue.dma_start(out=dst[:], in_=vec.rearrange("(g p j) -> p g j", g=GROUPS, j=PACK))
@@ -237,111 +265,125 @@ def tile_marginbradleyterryrewardmlpweightgradien_x2_kernel(
             ):
                 nc.vector.tensor_scalar(out=dst, in0=flat, scalar1=factor, scalar2=None, op0=ALU.mult)
 
-        nc.vector.memset(w_scales[:].rearrange("p g n -> p (g n)").bitcast(I32), 0)
         nc.vector.memset(v_row[:], 0.0)
-        nc.vector.memset(ones[:], 1.0)
+        nc.vector.memset(w_scales[:].rearrange("p g n -> p (g n)").bitcast(I32), 0)
+        nc.vector.memset(warm[:], 0.0)
+        nc.vector.memset(ones[:], 0.5)
+        load_vector(nc.gpsimd, s_bf[0], sc)
+        nc.gpsimd.dma_start(out=v_row[0:1, :], in_=v.rearrange("(o f) -> o f", o=1))
         make_identity(nc, ident[:])
         load_rows(0, 0, 1)
-        load_vector(nc.scalar, s_bf[0], sc)
+        load_rows(0, 1, 2)
         nc.sync.dma_start(
             out=w_words[:].bitcast(I32), in_=w1_words.rearrange("g p n -> p g n").bitcast(I32)
         )
+        load_rows(0, 2, 4)
         for q in range(4):
             nc.scalar.dma_start(
                 out=w_scales[32 * q : 32 * q + 4, :, :].bitcast(I32),
                 in_=w1_scales[:, 4 * q : 4 * q + 4, :].rearrange("g r n -> r g n").bitcast(I32),
             )
-        for j in range(1, PACK):
-            load_rows(0, j, j + 1)
+        nc.scalar.activation(out=warm[:], in_=warm[:], func=ACT.Silu)
         for b in range(1, BLOCKS):
             load_rows(b, 0, 2)
             load_rows(b, 2, 4)
-        nc.gpsimd.dma_start(out=v_row[0:1, :], in_=v.rearrange("(o f) -> o f", o=1))
         load_vector(nc.gpsimd, s_bf[1], sr)
         load_vector(nc.gpsimd, m_bf, m)
 
         transposes(0)
         transposes(1)
-        unload_t(0, True)
-        row_scales(0)
+        unload_t(0, False)
+        unload_t(1, False)
         quant_t(0)
+        row_scales(0)
         forward(0)
         transposes(2)
         for half in range(2):
             cols = slice(BANK * half, BANK * (half + 1))
             nc.tensor.matmul(v_all[:, cols], lhsT=ones[:], rhs=v_row[:, cols], start=True, stop=True)
-        transposes(3)
-        unload_t(1, True)
-        unload_t(2, True)
+        weave_h(0, True)
         quant_t(1)
         forward(1)
-        quant_t(2)
-        forward(2)
-        unload_t(3, True)
-        row_scales(1)
+        weave_h(1, True)
+        nc.vector.tensor_scalar(
+            out=v_pool[:], in0=v_all[:, 0:POOL_COLS], scalar1=2.0, scalar2=None, op0=ALU.mult
+        )
 
+        piece = 2
+        quantised = 0
         for s in range(TILES):
             activate(s, ACT.Silu, u_t, s_full)
             op_w(s)
-            if s >= 1:
-                op_y(s - 1)
-                if s + 3 < TILES:
-                    unload_t(s + 3, False)
-            if s + 4 < TILES:
-                transposes(s + 4)
+            if s == 0:
+                row_scales(1)
+            else:
+                op_y(s - 1, POOL_COLS)
+            if s + 2 < TILES:
+                unload_t(s + 2, False)
             if s + 3 < TILES:
-                quant_t(s + 3)
+                transposes(s + 3)
+            if s + 2 < TILES:
+                quant_t(s + 2)
+                forward(s + 2)
             activate(s, ACT.Tanh, t_t, s_half)
-            if s + 3 < TILES:
-                forward(s + 3)
             if s == TILES - 2:
                 nc.vector.scalar_tensor_tensor(
-                    out=part[:], in0=sums[:, 0, :], scalar=-INV_SQRT_F, in1=m_bf[:].rearrange("p g j -> p (g j)"),
-                    op0=ALU.mult, op1=ALU.add,
+                    out=part[:], in0=sums[:, 0, :], scalar=-2.0 * INV_SQRT_F,
+                    in1=m_bf[:].rearrange("p g j -> p (g j)"), op0=ALU.mult, op1=ALU.add,
                 )
             if s == TILES - 1:
                 nc.vector.scalar_tensor_tensor(
-                    out=logit[:], in0=sums[:, 1, :], scalar=INV_SQRT_F, in1=part[:], op0=ALU.mult, op1=ALU.add
+                    out=logit[:], in0=sums[:, 1, :], scalar=2.0 * INV_SQRT_F, in1=part[:], op0=ALU.mult, op1=ALU.add
                 )
                 nc.scalar.activation(out=sig[:], in_=logit[:], func=ACT.Sigmoid)
+            if piece >= PIECES * (quantised + 1) and quantised not in LATE_QUANT:
+                quant_h(quantised)
+                quantised += 1
+            if PLAN[s] != "-":
+                weave_h(piece, PLAN[s] == "V")
+                piece += 1
             op_x(s)
-            if 2 <= s < 2 + 3 * PIECES:
-                weave_h(s - 2)
-            if s in (6, 10):
-                quant_h((s - 6) // PIECES)
-        quant_h(2)
-        op_y(TILES - 1)
+            if s + 1 < TILES:
+                op_y_pool(s)
         nc.vector.tensor_tensor(
             out=row_factor[:],
             in0=s_signed[:],
             in1=sig[:].rearrange("p (a c) -> p a c", a=1).to_broadcast([P, 2, GROUPS * PACK]),
             op=ALU.mult,
         )
-        for piece in range(3 * PIECES, 4 * PIECES):
-            weave_h(piece)
+        op_y(TILES - 1, 0)
 
-        steps = CHUNKS * BLOCKS
+        steps = len(WIDTHS) * BLOCKS
+        passes = 0
         for q in range(steps + 1):
-            c, b = divmod(q, BLOCKS)
             if q < steps:
                 make_g(q)
-            if q == BLOCKS:
-                quant_h(BLOCKS - 1)
+            while piece < min(BLOCKS, quantised + 2) * PIECES:
+                weave_h(piece, False)
+                piece += 1
+            if LATE_QUANT.get(quantised) == q:
+                quant_h(quantised)
+                quantised += 1
             if q >= 1:
                 quant_g(q - 1)
-                backward(q - 1)
-            if b == 0 and 1 <= c < CHUNKS:
-                unload_out(2 * (c - 1), False)
-                unload_out(2 * (c - 1) + 1, False)
-                weave_out(2 * (c - 1), False)
-                weave_out(2 * (c - 1) + 1, False)
-            if b == 3 and c >= 1:
-                quant_out(2 * (c - 1))
-            if b == 0 and c >= 2:
-                quant_out(2 * (c - 2) + 1)
-        last = 2 * (CHUNKS - 1)
+            while passes < q and passes % BLOCKS < quantised:
+                backward(passes)
+                passes += 1
+                if passes % BLOCKS == 0 and passes < steps:
+                    r = GROUPS * (passes // BLOCKS - 1)
+                    unload_out(r, False)
+                    unload_out(r + 1, False)
+                    weave_out(r, False)
+                    weave_out(r + 1, False)
+            for r in OUT_QUANT:
+                if OUT_QUANT[r] == q and q < steps:
+                    quant_out(r)
+        last = GROUPS * (len(WIDTHS) - 1)
         unload_out(last, False)
         weave_out(last, False)
+        for r in OUT_QUANT:
+            if OUT_QUANT[r] == steps:
+                quant_out(r)
         unload_out(last + 1, True)
         weave_out(last + 1, True)
         quant_out(last)

@@ -24,11 +24,14 @@ TILES = BLOCKS * PACK
 BANK = 512
 INV_SQRT_F = 1.0 / 32.0
 CHUNK = 256
-WIDTHS = (256, 256, 256, 128, 128)
+WIDTHS = (256, 256, 256, 256)
 G_RING = 8
-PLAN = "V-S-S-S-S-S-S-SS"
+HEAD3 = True
+OUT_WEAVE_V = {5: 16}
+POOL_G = {256: 48, 128: 0}
+PLAN = "--S--S-V-S--S-SS"
 LATE_QUANT = {2: 1, 3: 4}
-OUT_QUANT = {0: 8, 1: 9, 2: 12, 3: 13, 4: 18, 5: 19, 6: 20, 7: 20}
+OUT_QUANT = {0: 8, 1: 9, 2: 12, 3: 13, 4: 16, 5: 16}
 PIECES = 4
 RUN = 4
 POOL_COLS = 640
@@ -188,13 +191,27 @@ def tile_marginbradleyterryrewardmlpweightgradien_x2_kernel(
         def make_g(q):
             c, b = divmod(q, BLOCKS)
             width = WIDTHS[c]
-            k4 = row_factor[:, side_of(b), PACK * (b // 2) : PACK * (b // 2 + 1)]
-            nc.vector.tensor_tensor(
-                out=g_bf[q % 3][:, 0 : PACK * width].rearrange("p (c i j) -> p c j i", i=RUN, j=PACK),
-                in0=y_t[b][:, :, chunk_cols(c)].rearrange("p j (c i) -> p c j i", i=RUN),
-                in1=k4.rearrange("p (a j e) -> p a j e", a=1, e=1).to_broadcast([P, width // RUN, PACK, RUN]),
-                op=ALU.mult,
-            )
+            split = POOL_G[width]
+            first = GROUPS * PACK * side_of(b) + PACK * (b // 2)
+            for engine, factors, lo, hi in (
+                (nc.gpsimd, row_factor[:].rearrange("p a c -> p (a c)"), 0, split),
+                (nc.vector, banks[6], split, width),
+            ):
+                if hi == lo:
+                    continue
+                k4 = factors[:, first : first + PACK].rearrange("p (a j e) -> p a j e", a=1, e=1)
+                cols = slice(chunk_cols(c).start + lo, chunk_cols(c).start + hi)
+                engine.tensor_tensor(
+                    out=g_bf[q % 3][:, PACK * lo : PACK * hi].rearrange("p (c i j) -> p c j i", i=RUN, j=PACK),
+                    in0=y_t[b][:, :, cols].rearrange("p j (c i) -> p c j i", i=RUN),
+                    in1=k4.to_broadcast([P, (hi - lo) // RUN, PACK, RUN]),
+                    op=ALU.mult,
+                )
+
+        def out_sum(i, width):
+            if i < 6:
+                return banks[i][:, 0:width]
+            return banks[7][:, CHUNK * (i - 6) : CHUNK * (i - 6) + width]
 
         def quant_g(q):
             width = WIDTHS[q // BLOCKS]
@@ -204,26 +221,32 @@ def tile_marginbradleyterryrewardmlpweightgradien_x2_kernel(
                 in_=g_bf[q % 3][:, 0 : PACK * width],
             )
 
-        def backward(q):
+        def backward_pass(q, i):
             c, b = divmod(q, BLOCKS)
             width = WIDTHS[c]
-            for i in range(8):
-                nc.tensor.matmul_mx(
-                    out=banks[i][:, 0:width],
-                    lhsT=hn_codes[b][:, i * P : (i + 1) * P].bitcast(FP8X4),
-                    lhsT_scale=hn_scales[b][:, i * P : (i + 1) * P],
-                    rhs=g_codes[q % G_RING][:, 0:width].bitcast(FP8X4),
-                    rhs_scale=g_scales[q % G_RING][:, 0:width],
-                    start=(b == 0),
-                    stop=(b == BLOCKS - 1),
-                )
+            nc.tensor.matmul_mx(
+                out=out_sum(i, width),
+                lhsT=hn_codes[b][:, i * P : (i + 1) * P].bitcast(FP8X4),
+                lhsT_scale=hn_scales[b][:, i * P : (i + 1) * P],
+                rhs=g_codes[q % G_RING][:, 0:width].bitcast(FP8X4),
+                rhs_scale=g_scales[q % G_RING][:, 0:width],
+                start=(b == 0),
+                stop=(b == BLOCKS - 1),
+            )
+
+        def backward(q):
+            for i in range(7):
+                backward_pass(q, i)
+            if q % BLOCKS == BLOCKS - 1:
+                for earlier in range(q - BLOCKS + 1, q + 1):
+                    backward_pass(earlier, 7)
 
         def unload_out(r, on_vector):
             c, g = divmod(r, GROUPS)
             width = WIDTHS[c]
             for t in range(PACK):
                 dst = o_f32[r % 4][:, t, 0:width]
-                src = banks[PACK * g + t][:, 0:width]
+                src = out_sum(PACK * g + t, width)
                 if on_vector:
                     nc.vector.tensor_scalar(out=dst, in0=src, scalar1=INV_SQRT_F, scalar2=None, op0=ALU.mult)
                 else:
@@ -248,10 +271,16 @@ def tile_marginbradleyterryrewardmlpweightgradien_x2_kernel(
                 scales=o_scales[:, g, cols],
                 in_=o_bf[r % 4][:, 0 : PACK * WIDTHS[c]],
             )
-            if g == GROUPS - 1 and cols.stop % CHUNK == 0:
-                done = slice(cols.stop - CHUNK, cols.stop)
-                words = out_1.rearrange("g p f t -> p g (f t)")[:, :, PACK * done.start : PACK * done.stop]
-                nc.sync.dma_start(out=words.bitcast(I32), in_=o_codes[:, :, done].bitcast(I32))
+            if g == GROUPS - 1:
+                words = out_1.rearrange("g p f t -> p g (f t)")[:, :, PACK * cols.start : PACK * cols.stop]
+                nc.sync.dma_start(out=words.bitcast(I32), in_=o_codes[:, :, cols].bitcast(I32))
+
+        def load_w(half):
+            cols = slice(2 * BANK * half, 2 * BANK * (half + 1))
+            nc.sync.dma_start(
+                out=w_words[:, :, cols].bitcast(I32),
+                in_=w1_words.rearrange("g p n -> p g n")[:, :, cols].bitcast(I32),
+            )
 
         def load_vector(queue, dst, vec):
             queue.dma_start(out=dst[:], in_=vec.rearrange("(g p j) -> p g j", g=GROUPS, j=PACK))
@@ -265,24 +294,23 @@ def tile_marginbradleyterryrewardmlpweightgradien_x2_kernel(
             ):
                 nc.vector.tensor_scalar(out=dst, in0=flat, scalar1=factor, scalar2=None, op0=ALU.mult)
 
+        nc.vector.memset(ones[:], 0.5)
         nc.vector.memset(v_row[:], 0.0)
         nc.vector.memset(w_scales[:].rearrange("p g n -> p (g n)").bitcast(I32), 0)
         nc.vector.memset(warm[:], 0.0)
-        nc.vector.memset(ones[:], 0.5)
         load_vector(nc.gpsimd, s_bf[0], sc)
         nc.gpsimd.dma_start(out=v_row[0:1, :], in_=v.rearrange("(o f) -> o f", o=1))
         make_identity(nc, ident[:])
         load_rows(0, 0, 1)
+        load_w(0)
         load_rows(0, 1, 2)
-        nc.sync.dma_start(
-            out=w_words[:].bitcast(I32), in_=w1_words.rearrange("g p n -> p g n").bitcast(I32)
-        )
-        load_rows(0, 2, 4)
+        load_rows(0, 2, PACK)
         for q in range(4):
             nc.scalar.dma_start(
                 out=w_scales[32 * q : 32 * q + 4, :, :].bitcast(I32),
                 in_=w1_scales[:, 4 * q : 4 * q + 4, :].rearrange("g r n -> r g n").bitcast(I32),
             )
+        load_w(1)
         nc.scalar.activation(out=warm[:], in_=warm[:], func=ACT.Silu)
         for b in range(1, BLOCKS):
             load_rows(b, 0, 2)
@@ -293,30 +321,30 @@ def tile_marginbradleyterryrewardmlpweightgradien_x2_kernel(
         transposes(0)
         transposes(1)
         unload_t(0, False)
-        unload_t(1, False)
-        quant_t(0)
         row_scales(0)
+        quant_t(0)
         forward(0)
-        transposes(2)
+        unload_t(1, False)
         for half in range(2):
             cols = slice(BANK * half, BANK * (half + 1))
             nc.tensor.matmul(v_all[:, cols], lhsT=ones[:], rhs=v_row[:, cols], start=True, stop=True)
+        transposes(2)
         weave_h(0, True)
         quant_t(1)
         forward(1)
         weave_h(1, True)
-        nc.vector.tensor_scalar(
-            out=v_pool[:], in0=v_all[:, 0:POOL_COLS], scalar1=2.0, scalar2=None, op0=ALU.mult
-        )
+        weave_h(2, True)
+        weave_h(3, HEAD3)
+        row_scales(1)
 
-        piece = 2
+        piece = 4
         quantised = 0
         for s in range(TILES):
             activate(s, ACT.Silu, u_t, s_full)
-            op_w(s)
             if s == 0:
-                row_scales(1)
-            else:
+                nc.scalar.activation(out=v_pool[:], in_=v_all[:, 0:POOL_COLS], func=ACT.Copy, scale=2.0)
+            op_w(s)
+            if s >= 1:
                 op_y(s - 1, POOL_COLS)
             if s + 2 < TILES:
                 unload_t(s + 2, False)
@@ -351,6 +379,13 @@ def tile_marginbradleyterryrewardmlpweightgradien_x2_kernel(
             in1=sig[:].rearrange("p (a c) -> p a c", a=1).to_broadcast([P, 2, GROUPS * PACK]),
             op=ALU.mult,
         )
+        nc.tensor.matmul(
+            banks[6][:, 0 : 2 * GROUPS * PACK],
+            lhsT=ident[:],
+            rhs=row_factor[:].rearrange("p a c -> p (a c)"),
+            start=True,
+            stop=True,
+        )
         op_y(TILES - 1, 0)
 
         steps = len(WIDTHS) * BLOCKS
@@ -364,6 +399,12 @@ def tile_marginbradleyterryrewardmlpweightgradien_x2_kernel(
             if LATE_QUANT.get(quantised) == q:
                 quant_h(quantised)
                 quantised += 1
+            for r in OUT_WEAVE_V:
+                if OUT_WEAVE_V[r] == q and q < steps:
+                    weave_out(r, True)
+            for r in OUT_QUANT:
+                if OUT_QUANT[r] == q and q < steps:
+                    quant_out(r)
             if q >= 1:
                 quant_g(q - 1)
             while passes < q and passes % BLOCKS < quantised:
@@ -373,14 +414,15 @@ def tile_marginbradleyterryrewardmlpweightgradien_x2_kernel(
                     r = GROUPS * (passes // BLOCKS - 1)
                     unload_out(r, False)
                     unload_out(r + 1, False)
-                    weave_out(r, False)
-                    weave_out(r + 1, False)
-            for r in OUT_QUANT:
-                if OUT_QUANT[r] == q and q < steps:
-                    quant_out(r)
+                    for done in (r, r + 1):
+                        if done not in OUT_WEAVE_V:
+                            weave_out(done, False)
         last = GROUPS * (len(WIDTHS) - 1)
         unload_out(last, False)
         weave_out(last, False)
+        for r in OUT_WEAVE_V:
+            if OUT_WEAVE_V[r] == steps:
+                weave_out(r, True)
         for r in OUT_QUANT:
             if OUT_QUANT[r] == steps:
                 quant_out(r)

@@ -28,13 +28,13 @@ WIDTHS = (256, 256, 256, 256)
 G_RING = 8
 HEAD3 = True
 OUT_WEAVE_V = {5: 16}
-POOL_G = {256: 48, 128: 0}
+POOL_G = {256: 32, 128: 0}
 PLAN = "--S--S-V-S--S-SS"
 LATE_QUANT = {2: 1, 3: 4}
 OUT_QUANT = {0: 8, 1: 9, 2: 12, 3: 13, 4: 16, 5: 16}
 PIECES = 4
 RUN = 4
-POOL_COLS = 640
+POOL_COLS = 512
 
 
 def tile_marginbradleyterryrewardmlpweightgradien_x2_kernel(

from contextlib import ExitStack

import concourse.mybir as mybir
from concourse.masks import make_identity

N, D, F = 1024, 1024, 1024
FLOPS = 4 * 2 * N * D * F

F32 = mybir.dt.float32
BF16 = mybir.dt.bfloat16
I32 = mybir.dt.int32
U32 = mybir.dt.uint32
U8 = mybir.dt.uint8
FP8X4 = mybir.dt.float8_e4m3fn_x4
FP4X4 = mybir.dt.float4_e2m1fn_x4
ALU = mybir.AluOpType
ACT = mybir.ActivationFunctionType

P = 128
PACK = 4
GROUPS = 2
BLOCKS = 4
TILES = BLOCKS * PACK
BANK = 512
INV_SQRT_F = 1.0 / 32.0
CHUNK = 256
WIDTHS = (256, 256, 256, 256)
G_RING = 8
HEAD3 = True
OUT_WEAVE_V = {5: 16}
POOL_G = {256: 32, 128: 0}
PLAN = "--S--S-V-S--S-SS"
LATE_QUANT = {2: 1, 3: 4}
OUT_QUANT = {0: 8, 1: 9, 2: 12, 3: 13, 4: 16, 5: 16}
PIECES = 4
RUN = 4
POOL_COLS = 512


def tile_marginbradleyterryrewardmlpweightgradien_x2_kernel(
    tc, hc, hr, w1_words, w1_scales, v, sc, sr, m, out_0, out_1, out_2
):
    nc = tc.nc
    h_dram = (hc, hr)
    s_dram = (sc, sr)

    with ExitStack() as ctx:
        sb = ctx.enter_context(tc.tile_pool(name="sb", bufs=1))
        ps = ctx.enter_context(tc.psum_pool(name="ps", bufs=1))
        ctx.enter_context(tc.manual_schedule())

        def ring(name, count, shape, dtype):
            return [sb.tile(shape, dtype, name="%s%d" % (name, i), align_bytes=64) for i in range(count)]

        banks = [ps.tile([P, BANK], F32, name="bank%d" % i) for i in range(8)]
        raw = ring("raw", BLOCKS, [P, PACK, D], BF16)
        w_words = sb.tile([P, GROUPS, 2 * F], U8, align_bytes=64)
        w_scales = sb.tile([P, GROUPS, F], U8, align_bytes=64)
        ident = sb.tile([P, P], F32, align_bytes=64)
        v_pool = sb.tile([P, POOL_COLS], F32, align_bytes=64)
        warm = sb.tile([P, 1], F32, align_bytes=64)
        ones = sb.tile([P, P], BF16, align_bytes=64)
        v_row = sb.tile([P, F], BF16, align_bytes=64)
        s_bf = ring("s_bf", 2, [P, GROUPS, PACK], BF16)
        m_bf = sb.tile([P, GROUPS, PACK], BF16, align_bytes=64)
        s_full = ring("s_full", 2, [P, GROUPS * PACK], F32)
        s_half = ring("s_half", 2, [P, GROUPS * PACK], F32)
        s_signed = sb.tile([P, 2, GROUPS * PACK], F32, align_bytes=64)
        sums = sb.tile([P, 2, GROUPS * PACK], F32, align_bytes=64)
        part = sb.tile([P, GROUPS * PACK], F32, align_bytes=64)
        logit = sb.tile([P, GROUPS * PACK], F32, align_bytes=64)
        sig = sb.tile([P, GROUPS * PACK], F32, align_bytes=64)
        row_factor = sb.tile([P, 2, GROUPS * PACK], F32, align_bytes=64)
        ht = ring("ht", 2, [P, GROUPS * P * PACK], BF16)
        ht_codes = ring("ht_codes", 4, [P, GROUPS * P], U32)
        ht_scales = ring("ht_scales", 4, [P, GROUPS * P], U8)
        hn = ring("hn", 2, [P, D * PACK], BF16)
        hn_codes = ring("hn_codes", BLOCKS, [P, D], U32)
        hn_scales = ring("hn_scales", BLOCKS, [P, D], U8)
        u_t = ring("u_t", 3, [P, F], F32)
        t_t = ring("t_t", 3, [P, F], F32)
        y_t = ring("y_t", BLOCKS, [P, PACK, F], F32)
        g_bf = ring("g_bf", 3, [P, CHUNK * PACK], BF16)
        g_codes = ring("g_codes", G_RING, [P, CHUNK], U32)
        g_scales = ring("g_scales", G_RING, [P, CHUNK], U8)
        o_f32 = ring("o_f32", 4, [P, PACK, CHUNK], F32)
        o_bf = ring("o_bf", 4, [P, CHUNK * PACK], BF16)
        o_codes = sb.tile([P, GROUPS, F], U32, align_bytes=64)
        o_scales = sb.tile([P, GROUPS, F], U8, align_bytes=64)

        v_all = banks[7][:].bitcast(BF16)

        def t_bank(t):
            return banks[2] if t == 1 else banks[6]

        def side_of(b):
            return b % 2

        def col_of(t):
            return (t // PACK // 2) * PACK + t % PACK

        def load_rows(b, j0, j1):
            rows = h_dram[side_of(b)][(b // 2) * 512 : (b // 2 + 1) * 512, :].rearrange("(p j) d -> p j d", j=PACK)
            nc.sync.dma_start(out=raw[b][:, j0:j1, :], in_=rows[:, j0:j1, :])

        def transposes(t):
            words = raw[t // PACK][:, t % PACK, :].bitcast(F32)
            bank = t_bank(t)
            for g in range(GROUPS):
                for u in range(2):
                    q = 2 * g + u
                    nc.tensor.transpose(
                        bank[:, q * P : (q + 1) * P], words[:, 256 * g + u : 256 * (g + 1) : 2], ident[:]
                    )

        def unload_t(t, on_vector):
            src = t_bank(t)[:].rearrange("p (g u n) -> p g n u", g=GROUPS, u=2)
            dst = ht[t % 2][:].bitcast(F32).rearrange("p (g n u) -> p g n u", g=GROUPS, u=2)
            if on_vector:
                nc.vector.tensor_copy(out=dst, in_=src)
            else:
                nc.scalar.copy(out=dst, in_=src)

        def quant_t(t):
            nc.vector.quantize_mx(out=ht_codes[t % 4][:].bitcast(FP8X4), scales=ht_scales[t % 4][:], in_=ht[t % 2][:])

        def forward(t):
            for half in range(2):
                for g in range(GROUPS):
                    nc.tensor.matmul_mx(
                        out=banks[2 * (t % 3) + half][:],
                        lhsT=ht_codes[t % 4][:, g * P : (g + 1) * P].bitcast(FP8X4),
                        lhsT_scale=ht_scales[t % 4][:, g * P : (g + 1) * P],
                        rhs=w_words[:, g, 2 * BANK * half : 2 * BANK * (half + 1)].bitcast(FP4X4),
                        rhs_scale=w_scales[:, g, BANK * half : BANK * (half + 1)],
                        start=(g == 0),
                        stop=(g == GROUPS - 1),
                    )

        def activate(t, func, dst, scales):
            c = col_of(t)
            for half in range(2):
                nc.scalar.activation(
                    out=dst[t % 3][:, BANK * half : BANK * (half + 1)],
                    in_=banks[2 * (t % 3) + half][:],
                    func=func,
                    scale=scales[side_of(t // PACK)][:, c : c + 1],
                )

        def op_w(t):
            c = col_of(t)
            nc.vector.scalar_tensor_tensor(
                out=u_t[t % 3][:], in0=u_t[t % 3][:], scalar=1.0, in1=v_all, op0=ALU.subtract, op1=ALU.mult,
                accum_out=sums[:, side_of(t // PACK), c : c + 1],
            )

        def op_x(t):
            nc.vector.scalar_tensor_tensor(
                out=t_t[t % 3][:], in0=t_t[t % 3][:], scalar=1.0, in1=u_t[t % 3][:], op0=ALU.subtract, op1=ALU.mult
            )

        def op_y(t, first):
            nc.vector.scalar_tensor_tensor(
                out=y_t[t // PACK][:, t % PACK, first:F], in0=v_all[:, first:F], scalar=2.0,
                in1=t_t[t % 3][:, first:F], op0=ALU.mult, op1=ALU.subtract,
            )

        def op_y_pool(t):
            nc.gpsimd.tensor_tensor(
                out=y_t[t // PACK][:, t % PACK, 0:POOL_COLS], in0=v_pool[:], in1=t_t[t % 3][:, 0:POOL_COLS],
                op=ALU.subtract,
            )

        def weave_h(piece, on_vector):
            b, q = divmod(piece, PIECES)
            g, half = divmod(q, 2)
            ms = slice(64 * half, 64 * (half + 1))
            src = raw[b][:, :, 512 * g : 512 * (g + 1)].rearrange("p j (m t) -> p m t j", t=PACK)
            dst = hn[b % 2][:, 2048 * g : 2048 * (g + 1)].rearrange("p (t m j) -> p m t j", t=PACK, j=PACK)
            if on_vector:
                nc.vector.tensor_copy(out=dst[:, ms, :, :], in_=src[:, ms, :, :])
            else:
                nc.scalar.copy(out=dst[:, ms, :, :], in_=src[:, ms, :, :])

        def quant_h(b):
            nc.vector.quantize_mx(out=hn_codes[b][:].bitcast(FP8X4), scales=hn_scales[b][:], in_=hn[b % 2][:])

        def chunk_cols(c):
            return slice(sum(WIDTHS[:c]), sum(WIDTHS[: c + 1]))

        def make_g(q):
            c, b = divmod(q, BLOCKS)
            width = WIDTHS[c]
            split = POOL_G[width]
            first = GROUPS * PACK * side_of(b) + PACK * (b // 2)
            for engine, factors, lo, hi in (
                (nc.gpsimd, row_factor[:].rearrange("p a c -> p (a c)"), 0, split),
                (nc.vector, banks[6], split, width),
            ):
                if hi == lo:
                    continue
                k4 = factors[:, first : first + PACK].rearrange("p (a j e) -> p a j e", a=1, e=1)
                cols = slice(chunk_cols(c).start + lo, chunk_cols(c).start + hi)
                engine.tensor_tensor(
                    out=g_bf[q % 3][:, PACK * lo : PACK * hi].rearrange("p (c i j) -> p c j i", i=RUN, j=PACK),
                    in0=y_t[b][:, :, cols].rearrange("p j (c i) -> p c j i", i=RUN),
                    in1=k4.to_broadcast([P, (hi - lo) // RUN, PACK, RUN]),
                    op=ALU.mult,
                )

        def out_sum(i, width):
            if i < 6:
                return banks[i][:, 0:width]
            return banks[7][:, CHUNK * (i - 6) : CHUNK * (i - 6) + width]

        def quant_g(q):
            width = WIDTHS[q // BLOCKS]
            nc.vector.quantize_mx(
                out=g_codes[q % G_RING][:, 0:width].bitcast(FP8X4),
                scales=g_scales[q % G_RING][:, 0:width],
                in_=g_bf[q % 3][:, 0 : PACK * width],
            )

        def backward_pass(q, i):
            c, b = divmod(q, BLOCKS)
            width = WIDTHS[c]
            nc.tensor.matmul_mx(
                out=out_sum(i, width),
                lhsT=hn_codes[b][:, i * P : (i + 1) * P].bitcast(FP8X4),
                lhsT_scale=hn_scales[b][:, i * P : (i + 1) * P],
                rhs=g_codes[q % G_RING][:, 0:width].bitcast(FP8X4),
                rhs_scale=g_scales[q % G_RING][:, 0:width],
                start=(b == 0),
                stop=(b == BLOCKS - 1),
            )

        def backward(q):
            for i in range(7):
                backward_pass(q, i)
            if q % BLOCKS == BLOCKS - 1:
                for earlier in range(q - BLOCKS + 1, q + 1):
                    backward_pass(earlier, 7)

        def unload_out(r, on_vector):
            c, g = divmod(r, GROUPS)
            width = WIDTHS[c]
            for t in range(PACK):
                dst = o_f32[r % 4][:, t, 0:width]
                src = out_sum(PACK * g + t, width)
                if on_vector:
                    nc.vector.tensor_scalar(out=dst, in0=src, scalar1=INV_SQRT_F, scalar2=None, op0=ALU.mult)
                else:
                    nc.scalar.activation(out=dst, in_=src, func=ACT.Copy, scale=INV_SQRT_F)
            rows = out_0[512 * g : 512 * (g + 1), chunk_cols(c)].rearrange("(p t) f -> p t f", t=PACK)
            nc.sync.dma_start(out=rows, in_=o_f32[r % 4][:, :, 0:width])

        def weave_out(r, on_vector):
            width = WIDTHS[r // GROUPS]
            src = o_f32[r % 4][:, :, 0:width].rearrange("p t (c i) -> p c t i", i=RUN)
            dst = o_bf[r % 4][:, 0 : PACK * width].rearrange("p (c i t) -> p c t i", i=RUN, t=PACK)
            if on_vector:
                nc.vector.tensor_copy(out=dst, in_=src)
            else:
                nc.scalar.copy(out=dst, in_=src)

        def quant_out(r):
            c, g = divmod(r, GROUPS)
            cols = chunk_cols(c)
            nc.vector.quantize_mx(
                out=o_codes[:, g, cols].bitcast(FP8X4),
                scales=o_scales[:, g, cols],
                in_=o_bf[r % 4][:, 0 : PACK * WIDTHS[c]],
            )
            if g == GROUPS - 1:
                words = out_1.rearrange("g p f t -> p g (f t)")[:, :, PACK * cols.start : PACK * cols.stop]
                nc.sync.dma_start(out=words.bitcast(I32), in_=o_codes[:, :, cols].bitcast(I32))

        def load_w(half):
            cols = slice(2 * BANK * half, 2 * BANK * (half + 1))
            nc.sync.dma_start(
                out=w_words[:, :, cols].bitcast(I32),
                in_=w1_words.rearrange("g p n -> p g n")[:, :, cols].bitcast(I32),
            )

        def load_vector(queue, dst, vec):
            queue.dma_start(out=dst[:], in_=vec.rearrange("(g p j) -> p g j", g=GROUPS, j=PACK))

        def row_scales(side):
            flat = s_bf[side][:].rearrange("p g j -> p (g j)")
            for dst, factor in (
                (s_full[side][:], 1.0),
                (s_half[side][:], 0.5),
                (s_signed[:, side, :], 2.0 * side - 1.0),
            ):
                nc.vector.tensor_scalar(out=dst, in0=flat, scalar1=factor, scalar2=None, op0=ALU.mult)

        nc.vector.memset(ones[:], 0.5)
        nc.vector.memset(v_row[:], 0.0)
        nc.vector.memset(w_scales[:].rearrange("p g n -> p (g n)").bitcast(I32), 0)
        nc.vector.memset(warm[:], 0.0)
        load_vector(nc.gpsimd, s_bf[0], sc)
        nc.gpsimd.dma_start(out=v_row[0:1, :], in_=v.rearrange("(o f) -> o f", o=1))
        make_identity(nc, ident[:])
        load_rows(0, 0, 1)
        load_w(0)
        load_rows(0, 1, 2)
        load_rows(0, 2, PACK)
        for q in range(4):
            nc.scalar.dma_start(
                out=w_scales[32 * q : 32 * q + 4, :, :].bitcast(I32),
                in_=w1_scales[:, 4 * q : 4 * q + 4, :].rearrange("g r n -> r g n").bitcast(I32),
            )
        load_w(1)
        nc.scalar.activation(out=warm[:], in_=warm[:], func=ACT.Silu)
        for b in range(1, BLOCKS):
            load_rows(b, 0, 2)
            load_rows(b, 2, 4)
        load_vector(nc.gpsimd, s_bf[1], sr)
        load_vector(nc.gpsimd, m_bf, m)

        transposes(0)
        transposes(1)
        unload_t(0, False)
        row_scales(0)
        quant_t(0)
        forward(0)
        unload_t(1, False)
        for half in range(2):
            cols = slice(BANK * half, BANK * (half + 1))
            nc.tensor.matmul(v_all[:, cols], lhsT=ones[:], rhs=v_row[:, cols], start=True, stop=True)
        transposes(2)
        weave_h(0, True)
        quant_t(1)
        forward(1)
        weave_h(1, True)
        weave_h(2, True)
        weave_h(3, HEAD3)
        row_scales(1)

        piece = 4
        quantised = 0
        for s in range(TILES):
            activate(s, ACT.Silu, u_t, s_full)
            if s == 0:
                nc.scalar.activation(out=v_pool[:], in_=v_all[:, 0:POOL_COLS], func=ACT.Copy, scale=2.0)
            op_w(s)
            if s >= 1:
                op_y(s - 1, POOL_COLS)
            if s + 2 < TILES:
                unload_t(s + 2, False)
            if s + 3 < TILES:
                transposes(s + 3)
            if s + 2 < TILES:
                quant_t(s + 2)
                forward(s + 2)
            activate(s, ACT.Tanh, t_t, s_half)
            if s == TILES - 2:
                nc.vector.scalar_tensor_tensor(
                    out=part[:], in0=sums[:, 0, :], scalar=-2.0 * INV_SQRT_F,
                    in1=m_bf[:].rearrange("p g j -> p (g j)"), op0=ALU.mult, op1=ALU.add,
                )
            if s == TILES - 1:
                nc.vector.scalar_tensor_tensor(
                    out=logit[:], in0=sums[:, 1, :], scalar=2.0 * INV_SQRT_F, in1=part[:], op0=ALU.mult, op1=ALU.add
                )
                nc.scalar.activation(out=sig[:], in_=logit[:], func=ACT.Sigmoid)
            if piece >= PIECES * (quantised + 1) and quantised not in LATE_QUANT:
                quant_h(quantised)
                quantised += 1
            if PLAN[s] != "-":
                weave_h(piece, PLAN[s] == "V")
                piece += 1
            op_x(s)
            if s + 1 < TILES:
                op_y_pool(s)
        nc.vector.tensor_tensor(
            out=row_factor[:],
            in0=s_signed[:],
            in1=sig[:].rearrange("p (a c) -> p a c", a=1).to_broadcast([P, 2, GROUPS * PACK]),
            op=ALU.mult,
        )
        nc.tensor.matmul(
            banks[6][:, 0 : 2 * GROUPS * PACK],
            lhsT=ident[:],
            rhs=row_factor[:].rearrange("p a c -> p (a c)"),
            start=True,
            stop=True,
        )
        op_y(TILES - 1, 0)

        steps = len(WIDTHS) * BLOCKS
        passes = 0
        for q in range(steps + 1):
            if q < steps:
                make_g(q)
            while piece < min(BLOCKS, quantised + 2) * PIECES:
                weave_h(piece, False)
                piece += 1
            if LATE_QUANT.get(quantised) == q:
                quant_h(quantised)
                quantised += 1
            for r in OUT_WEAVE_V:
                if OUT_WEAVE_V[r] == q and q < steps:
                    weave_out(r, True)
            for r in OUT_QUANT:
                if OUT_QUANT[r] == q and q < steps:
                    quant_out(r)
            if q >= 1:
                quant_g(q - 1)
            while passes < q and passes % BLOCKS < quantised:
                backward(passes)
                passes += 1
                if passes % BLOCKS == 0 and passes < steps:
                    r = GROUPS * (passes // BLOCKS - 1)
                    unload_out(r, False)
                    unload_out(r + 1, False)
                    for done in (r, r + 1):
                        if done not in OUT_WEAVE_V:
                            weave_out(done, False)
        last = GROUPS * (len(WIDTHS) - 1)
        unload_out(last, False)
        weave_out(last, False)
        for r in OUT_WEAVE_V:
            if OUT_WEAVE_V[r] == steps:
                weave_out(r, True)
        for r in OUT_QUANT:
            if OUT_QUANT[r] == steps:
                quant_out(r)
        unload_out(last + 1, True)
        weave_out(last + 1, True)
        quant_out(last)
        quant_out(last + 1)
        for q in range(4):
            queue = nc.scalar if q % 2 == 0 else nc.sync
            queue.dma_start(
                out=out_2[:, 4 * q : 4 * q + 4, :].rearrange("g r n -> r g n").bitcast(I32),
                in_=o_scales[32 * q : 32 * q + 4, :, :].bitcast(I32),
            )
